import numpy as np
import ml_dtypes


def mxq(x, axis, fmt="e4m3"):
    dtype, down = {"e4m3": (ml_dtypes.float8_e4m3fn, 7), "e5m2": (ml_dtypes.float8_e5m2, 14)}[fmt]
    v = np.moveaxis(np.asarray(x, np.float32).astype(ml_dtypes.bfloat16).astype(np.float64), axis, -1)
    blocks = v.reshape(v.shape[:-1] + (-1, 32))
    amax = np.abs(blocks).max(-1, keepdims=True)
    byte = np.maximum(np.where(amax > 0, np.frexp(amax)[1] - 1 + 127, 0) - down, 1)
    scale = np.exp2(byte - 127.0)
    codes = (blocks / scale).astype(np.float32).astype(dtype).astype(np.float64)
    return np.moveaxis((codes * scale).reshape(v.shape), -1, axis)


WIDE = False


def mx_kscale(k):
    if not WIDE:
        return np.ones(k)
    levels = np.array([10, -10, 5, -5, 0])
    if k % 512:
        return np.exp2(np.random.permutation(np.resize(levels, k // 32))).repeat(32)
    a = np.empty((k // 512, 16))
    for p in range(k // 512):
        a[p, :8] = np.random.permutation(np.resize(levels, 8))
        for g in range(8):
            far = levels[np.abs(levels - a[p, g]) >= 10]
            a[p, g + 8] = far[np.random.randint(len(far))]
    return np.exp2(a.ravel()).repeat(32)


def f64(x):
    return np.asarray(x).astype(np.float64)


def striped(idx):
    return np.tile(idx.reshape(-1, 16).T, (8, 1)).astype(np.uint16)


def unstriped(offs):
    return offs[:16].T.reshape(-1).astype(np.int64)


def pack_weight(w):
    k, n = w.shape
    w = f64(np.asarray(w, np.float32).astype(ml_dtypes.bfloat16)).reshape(k // 32, 32, n)
    amax = np.abs(w).max(1)
    byte = np.clip(np.where(amax > 0, np.frexp(amax)[1] - 1 + 127 - 7, 1), 1, 254)
    scaled = (w * np.exp2(127.0 - byte)[:, None, :]).reshape(k, n).astype(np.float32)
    words = np.ascontiguousarray(scaled.reshape(k // 512, 128, 4, n).transpose(0, 1, 3, 2)).astype(ml_dtypes.float8_e4m3fn).view(np.uint8)
    return words, np.ascontiguousarray(byte.astype(np.uint8).reshape(k // 512, 16, n))


def unpack_weight(words, scales):
    g, p, n, _ = words.shape
    vals = np.ascontiguousarray(words).view(ml_dtypes.float8_e4m3fn).astype(np.float64) * np.repeat(np.exp2(scales.astype(np.float64) - 127.0), 8, axis=1)[..., None]
    return vals.transpose(0, 1, 3, 2).reshape(g * 512, n)


K, T, S, D, N, H, V, U = 512, 4096, 1024, 4, 128, 512, 256, 512


def setup_inputs():
    n = np.random.standard_normal
    s = mx_kscale(K)[:, None]
    u = mx_kscale(H)
    packed_xT = pack_weight(n((K, T)) * s)
    return {
        "x_words": packed_xT[0],
        "x_scales": packed_xT[1],
        "w1": (n((K, H)) / np.sqrt(K) / s).astype(np.float32),
        "w2": (n((K, H)) / np.sqrt(K) / s).astype(np.float32),
        "loss": (np.random.uniform(0.0, 2.0, (H, S))).astype(np.float32),
        "exp_": (np.random.uniform(0.3, 1.0, (H, S))).astype(np.float32),
        "wt": (np.random.uniform(0.5, 1.5, (H, U))).astype(np.float32),
        "unit": (np.random.uniform(0.6, 1.4, (H, 1)) * u[:, None]).astype(np.float32),
        "w3": (n((H, N)) / np.sqrt(H) / u[:, None]).astype(np.float32),
        "offs": striped(np.random.permutation(T)[:S]),
        "seg": striped(np.random.permutation(np.concatenate([np.arange(V), np.random.randint(0, V, U - V)]))),
    }


def reference(x_words, x_scales, w1, w2, loss, exp_, wt, unit, w3, offs, seg):
    xq = unpack_weight(x_words, x_scales)[:, unstriped(offs)]
    mu = mxq(f64(w1), 0, "e4m3").T @ xq
    mean_ = np.exp(1.6 * np.tanh(mu))
    rtmu = np.sqrt(mean_)
    devi = f64(loss) / rtmu + rtmu - (2.0 * f64(exp_))
    ph = mxq(f64(w2), 0, "e4m3").T @ xq
    disp = np.log(np.exp(ph) + 1.0) + 0.3
    wd = devi / disp
    grp = wd.reshape(len(wd), -1, D).mean(axis=2)
    gs = grp[:, unstriped(seg)]
    lfi = np.log(disp)
    lmean = lfi.reshape(len(lfi), -1, D).mean(axis=2)
    ls = lmean[:, unstriped(seg)]
    hid = f64(unit) * (gs * f64(wt) - ls)
    return mxq(f64(w3), 0, "e4m3").T @ mxq(hid, 0, "e4m3")

@@ -1,0 +1,326 @@
+import math
+from contextlib import ExitStack
+
+import concourse.mybir as mybir
+from concourse.masks import make_identity
+
+K, T, S, D, N, H, V, U = 512, 4096, 1024, 4, 128, 512, 256, 512
+FLOPS = 2 * K * H * S * 2 + 2 * H * N * U
+
+F32 = mybir.dt.float32
+BF16 = mybir.dt.bfloat16
+I32 = mybir.dt.int32
+U32 = mybir.dt.uint32
+U16 = mybir.dt.uint16
+U8 = mybir.dt.uint8
+FP8X4 = mybir.dt.float8_e4m3fn_x4
+ALU = mybir.AluOpType
+ACT = mybir.ActivationFunctionType
+
+P = 128
+PACK = 4
+HALF = 512
+VB = 2
+WINDOW = V + 32
+LN_FLOOR = 2.0 ** -60
+
+
+def tile_picked_ytweed_ll_p_kernel(
+    tc, x_words, x_scales, w1, w2, loss, exp_, wt, unit, w3, offs, seg, out
+):
+    nc = tc.nc
+    with ExitStack() as ctx:
+        keep = ctx.enter_context(tc.tile_pool(name="keep", bufs=1))
+        stage = ctx.enter_context(tc.tile_pool(name="stage", bufs=2))
+        work = ctx.enter_context(tc.tile_pool(name="work", bufs=2))
+        psum = ctx.enter_context(tc.psum_pool(name="psum", bufs=1))
+
+        def bank(b, name):
+            return psum.tile([P, HALF], F32, tag="bank%d" % b, name=name)
+
+        offs_sb = keep.tile([P, S // 16], U16, name="offs_sb")
+        nc.sync.dma_start(offs_sb[:], offs)
+
+        scale_table = keep.tile([P, T], U8, tag="bytes", name="scale_table", align_bytes=64)
+        nc.vector.memset(scale_table[:].bitcast(I32), 0)
+        for q in range(4):
+            nc.scalar.dma_start(
+                scale_table[32 * q : 32 * q + 4, :].bitcast(I32),
+                x_scales[0, 4 * q : 4 * q + 4, :].bitcast(I32),
+            )
+
+        w2_raw = stage.tile([P, PACK, H], F32, tag="raw", name="w2_raw")
+        nc.sync.dma_start(w2_raw[:], w2.rearrange("(p j) c -> p j c", j=PACK))
+        word_table = keep.tile([P, T], U32, tag="table", name="word_table", align_bytes=64)
+        nc.sync.dma_start(
+            word_table[:].bitcast(I32), x_words[0].rearrange("p n t -> p (n t)").bitcast(I32)
+        )
+        w1_raw = stage.tile([P, PACK, H], F32, tag="raw", name="w1_raw")
+        nc.sync.dma_start(w1_raw[:], w1.rearrange("(p j) c -> p j c", j=PACK))
+        seg_sb = keep.tile([P, U // 16], U16, name="seg_sb")
+        nc.sync.dma_start(seg_sb[:], seg)
+
+        ident = keep.tile([P, P], F32, name="ident")
+        make_identity(nc, ident[:])
+
+        grp_win = [keep.tile([P, WINDOW], F32, name="grp_win%d" % t) for t in range(PACK)]
+        log_win = [keep.tile([P, WINDOW], F32, name="log_win%d" % t) for t in range(PACK)]
+        for win in grp_win + log_win:
+            nc.vector.memset(win[:, V:WINDOW], 0.0)
+
+        def quantize_dealt(raw, sign, name, tag):
+            grouped = keep.tile([P, H * PACK], BF16, tag=tag, name=name + "_bf", align_bytes=64)
+            nc.vector.tensor_scalar(
+                out=grouped[:].rearrange("p (t m j) -> p m j t", t=PACK, j=PACK),
+                in0=raw[:].rearrange("p j (m t) -> p m j t", t=PACK),
+                scalar1=sign,
+                scalar2=None,
+                op0=ALU.mult,
+            )
+            codes = keep.tile([P, H], U32, name=name + "_codes", align_bytes=64)
+            scales = keep.tile([P, H], U8, name=name + "_scales", align_bytes=64)
+            nc.vector.quantize_mx(out=codes[:].bitcast(FP8X4), scales=scales[:], in_=grouped[:])
+            return codes, scales
+
+        picked_scales = keep.tile([P, S], U8, tag="picked", name="picked_scales", align_bytes=64)
+        nc.vector.tensor_copy(picked_scales[:], scale_table[:].indirect(offs_sb[:]))
+        x_sc = keep.tile([P, S], U8, name="x_sc", align_bytes=64)
+        nc.vector.tensor_copy(
+            x_sc[:].rearrange("p (b d v) -> p b v d", b=VB, d=D),
+            picked_scales[:].rearrange("p (b v d) -> p b v d", b=VB, d=D),
+        )
+        w2_codes, w2_scales = quantize_dealt(w2_raw, -1.0, "w2", "w2_bf")
+        x_codes = keep.tile([P, S], U32, tag="picked", name="x_codes", align_bytes=64)
+        x_cd = [x_codes[:, HALF * b : HALF * (b + 1)] for b in range(VB)]
+        for b in range(VB):
+            nc.vector.tensor_copy(
+                x_cd[b].rearrange("p (d v) -> p v d", d=D),
+                word_table[:].indirect(offs_sb[:, 32 * b : 32 * (b + 1)]),
+            )
+        w1_codes, w1_scales = quantize_dealt(w1_raw, 1.0, "w1", "table")
+
+        exp_rows = exp_.rearrange("(p t) j -> p t j", t=PACK)
+        loss_rows = loss.rearrange("(p t) j -> p t j", t=PACK)
+        neg2e = [keep.tile([P, 2, S], F32, name="neg2e%d" % u) for u in range(2)]
+        for u in range(2):
+            exp_raw = stage.tile([P, 2, S], F32, tag="raw", name="exp_raw%d" % u)
+            nc.sync.dma_start(exp_raw[:], exp_rows[:, 2 * u : 2 * u + 2, :])
+            nc.vector.tensor_scalar(
+                out=neg2e[u][:].rearrange("p t (b d v) -> p (t b) v d", b=VB, d=D),
+                in0=exp_raw[:].rearrange("p t (b v d) -> p (t b) v d", b=VB, d=D),
+                scalar1=-2.0,
+                scalar2=None,
+                op0=ALU.mult,
+            )
+        loss_sb = []
+        for u in range(2):
+            loss_raw = stage.tile([P, 2, S], F32, tag="raw", name="loss_raw%d" % u)
+            nc.sync.dma_start(loss_raw[:], loss_rows[:, 2 * u : 2 * u + 2, :])
+            loss_sb.append(loss_raw)
+        wt_sb = keep.tile([P, PACK, U], F32, tag="table", name="wt_sb", align_bytes=64)
+        nc.sync.dma_start(wt_sb[:], wt.rearrange("(p t) r -> p t r", t=PACK))
+
+        unit_sb = keep.tile([P, PACK], F32, tag="w2_bf", name="unit_sb", align_bytes=64)
+        nc.sync.dma_start(unit_sb[:], unit.rearrange("(p t) o -> p (t o)", t=PACK))
+        w3_raw = keep.tile([P, PACK, N], F32, tag="bytes", name="w3_raw", align_bytes=64)
+        nc.sync.dma_start(w3_raw[:], w3.rearrange("(p j) c -> p j c", j=PACK))
+        w3_bf = keep.tile([P, N * PACK], BF16, name="w3_bf", align_bytes=64)
+        nc.vector.tensor_copy(
+            w3_bf[:].rearrange("p (c i j) -> p c j i", i=4, j=PACK),
+            w3_raw[:].rearrange("p j (c i) -> p c j i", i=4),
+        )
+        w3_codes = keep.tile([P, N], U32, name="w3_codes", align_bytes=64)
+        w3_scales = keep.tile([P, N], U8, name="w3_scales", align_bytes=64)
+        nc.vector.quantize_mx(out=w3_codes[:].bitcast(FP8X4), scales=w3_scales[:], in_=w3_bf[:])
+        neg_unit = keep.tile([P, PACK], F32, name="neg_unit")
+        nc.vector.tensor_scalar(
+            out=neg_unit[:], in0=unit_sb[:], scalar1=-1.0 / D, scalar2=None, op0=ALU.mult
+        )
+
+        neg_ph = {}
+        neg_disp = [keep.tile([P, D, H], F32, name="neg_disp%d" % b) for b in range(VB)]
+        for b in range(VB):
+            for d in range(D):
+                acc = bank(D * b + d, "neg_ph%d%d" % (b, d))
+                cols = slice(HALF * b + P * d, HALF * b + P * (d + 1))
+                nc.tensor.matmul_mx(
+                    out=acc[:],
+                    lhsT=x_cd[b][:, P * d : P * (d + 1)].bitcast(FP8X4),
+                    lhsT_scale=x_sc[:, cols],
+                    rhs=w2_codes[:].bitcast(FP8X4),
+                    rhs_scale=w2_scales[:],
+                    start=True,
+                    stop=True,
+                )
+                nc.scalar.activation(neg_disp[b][:, d, :], acc[:], ACT.Sigmoid)
+                neg_ph[b, d] = acc
+        for b in range(VB):
+            for u in range(2):
+                pair = neg_disp[b][:, 2 * u : 2 * u + 2, :]
+                nc.scalar.activation(pair, pair, ACT.Ln, scale=math.exp(-0.3), bias=LN_FLOOR)
+        prod = keep.tile([P, VB, H], F32, tag="prod_tanh", name="prod")
+        pair_prod = []
+        for b in range(VB):
+            for d in range(D):
+                nc.vector.scalar_tensor_tensor(
+                    out=neg_disp[b][:, d, :],
+                    in0=neg_ph[b, d][:],
+                    scalar=-0.3,
+                    in1=neg_disp[b][:, d, :],
+                    op0=ALU.add,
+                    op1=ALU.min,
+                )
+            other = keep.tile([P, 2, H], F32, name="other%d" % b)
+            for u in range(2):
+                nc.vector.tensor_tensor(
+                    other[:, 1 - u, :], neg_disp[b][:, 2 * u, :], neg_disp[b][:, 2 * u + 1, :], ALU.mult
+                )
+            nc.vector.tensor_tensor(prod[:, b, :], other[:, 0, :], other[:, 1, :], ALU.mult)
+            pair_prod.append(other)
+        log_prod = keep.tile([P, VB, H], F32, name="log_prod")
+        nc.scalar.activation(log_prod[:], prod[:], ACT.Ln)
+        cof = []
+        for b in range(VB):
+            cofactor = keep.tile([P, D, H], F32, name="cof%d" % b)
+            for e in range(2):
+                nc.vector.tensor_tensor(
+                    cofactor[:, e:D:2, :], neg_disp[b][:, 1 - e : D : 2, :], pair_prod[b][:], ALU.mult
+                )
+            cof.append(cofactor)
+
+        inv_prod = keep.tile([P, PACK, V], F32, name="inv_prod")
+        for u in range(2):
+            turned = bank(2 + u, "log_turned%d" % u)
+            for tt in range(2):
+                t = 2 * u + tt
+                for b in range(VB):
+                    nc.tensor.transpose(
+                        turned[:, V * tt + P * b : V * tt + P * (b + 1)],
+                        log_prod[:, b, P * t : P * (t + 1)],
+                        ident[:],
+                    )
+            for tt in range(2):
+                nc.scalar.activation(
+                    log_win[2 * u + tt][:, 0:V], turned[:, V * tt : V * (tt + 1)], ACT.Copy
+                )
+            nc.scalar.activation(
+                inv_prod[:, 2 * u : 2 * u + 2, :].rearrange("p t v -> p (t v)"), turned[:], ACT.Exp, scale=-1.0
+            )
+
+        hid = keep.tile([P, PACK, U], F32, name="hid")
+        for t in range(PACK):
+            th = keep.tile([P, S], F32, tag="prod_tanh", name="th%d" % t)
+            for b in range(VB):
+                mu = bank(b, "mu%d%d" % (t, b))
+                nc.tensor.matmul_mx(
+                    out=mu[:],
+                    lhsT=w1_codes[:, P * t : P * (t + 1)].bitcast(FP8X4),
+                    lhsT_scale=w1_scales[:, P * t : P * (t + 1)],
+                    rhs=x_cd[b].bitcast(FP8X4),
+                    rhs_scale=x_sc[:, HALF * b : HALF * (b + 1)],
+                    start=True,
+                    stop=True,
+                )
+                nc.scalar.activation(th[:, HALF * b : HALF * (b + 1)], mu[:], ACT.Tanh)
+            inv_root = work.tile([P, S], F32, tag="inv_root", name="inv_root%d" % t)
+            root = work.tile([P, S], F32, tag="root", name="root%d" % t)
+            nc.scalar.activation(inv_root[:], th[:], ACT.Exp, scale=-0.8)
+            nc.scalar.activation(root[:], th[:], ACT.Exp, scale=0.8)
+            logs = work.tile([P, U], F32, tag="logs", name="logs%d" % t)
+            for h in range(2):
+                nc.scalar.activation(
+                    logs[:, V * h : V * (h + 1)],
+                    log_win[t][:].indirect(seg_sb[:, 16 * h : 16 * (h + 1)]),
+                    ACT.Copy,
+                )
+
+            ratio = work.tile([P, S], F32, tag="ratio", name="ratio%d" % t)
+            sums = bank(6 + t % 2, "sums%d" % t)
+            for b in range(VB):
+                half = slice(HALF * b, HALF * (b + 1))
+                nc.vector.tensor_tensor(
+                    ratio[:, half].rearrange("p (d c i) -> p c d i", d=D, i=4),
+                    loss_sb[t // 2][:, t % 2, half].rearrange("p (c i d) -> p c d i", d=D, i=4),
+                    inv_root[:, half].rearrange("p (d c i) -> p c d i", d=D, i=4),
+                    ALU.mult,
+                )
+            for b in range(VB):
+                devi = bank(4 - 2 * (t % 2) + b, "devi%d%d" % (t, b))
+                terms = [neg2e[t // 2][:, t % 2, :], root[:], ratio[:]]
+                for k, term in enumerate(terms):
+                    for d in range(D):
+                        nc.tensor.matmul(
+                            devi[:, P * d : P * (d + 1)],
+                            lhsT=term[:, HALF * b + P * d : HALF * b + P * (d + 1)],
+                            rhs=ident[:],
+                            start=(k == 0 and d == 0),
+                            stop=(k == len(terms) - 1 and d == D - 1),
+                            is_transpose=True,
+                        )
+                weighted = work.tile([P, D, P], F32, tag="weighted", name="weighted%d%d" % (t, b))
+                nc.vector.tensor_tensor(
+                    weighted[:],
+                    devi[:].rearrange("p (d i) -> p d i", d=D),
+                    cof[b][:, :, P * t : P * (t + 1)],
+                    ALU.mult,
+                )
+                for d in range(D):
+                    nc.tensor.matmul(
+                        sums[:, P * b : P * (b + 1)],
+                        lhsT=weighted[:, d, :],
+                        rhs=ident[:],
+                        start=(d == 0),
+                        stop=(d == D - 1),
+                        is_transpose=True,
+                    )
+            nc.vector.scalar_tensor_tensor(
+                out=grp_win[t][:, 0:V],
+                in0=sums[:, 0:V],
+                scalar=neg_unit[:, t : t + 1],
+                in1=inv_prod[:, t, :],
+                op0=ALU.mult,
+                op1=ALU.mult,
+            )
+            scaled = work.tile([P, U], F32, tag="scaled", name="scaled%d" % t)
+            for h in range(2):
+                cols = slice(V * h, V * (h + 1))
+                nc.vector.tensor_tensor(
+                    scaled[:, cols],
+                    grp_win[t][:].indirect(seg_sb[:, 16 * h : 16 * (h + 1)]),
+                    wt_sb[:, t, cols],
+                    ALU.mult,
+                )
+            for h in range(2):
+                cols = slice(V * h, V * (h + 1))
+                nc.vector.scalar_tensor_tensor(
+                    out=hid[:, t, cols],
+                    in0=logs[:, cols],
+                    scalar=neg_unit[:, t : t + 1],
+                    in1=scaled[:, cols],
+                    op0=ALU.mult,
+                    op1=ALU.add,
+                )
+
+        for h in range(2):
+            cols = slice(V * h, V * (h + 1))
+            hid_bf = work.tile([P, V * PACK], BF16, tag="hid_bf", name="hid_bf%d" % h, align_bytes=64)
+            nc.vector.tensor_copy(
+                hid_bf[:].rearrange("p (c i t) -> p c t i", i=4, t=PACK),
+                hid[:, :, cols].rearrange("p t (c i) -> p c t i", i=4),
+            )
+            hid_codes = work.tile([P, V], U32, tag="hid_codes", name="hid_codes%d" % h, align_bytes=64)
+            hid_scales = work.tile([P, V], U8, tag="hid_scales", name="hid_scales%d" % h, align_bytes=64)
+            nc.vector.quantize_mx(out=hid_codes[:].bitcast(FP8X4), scales=hid_scales[:], in_=hid_bf[:])
+            res = bank(h, "res%d" % h)
+            nc.tensor.matmul_mx(
+                out=res[:, 0:V],
+                lhsT=w3_codes[:].bitcast(FP8X4),
+                lhsT_scale=w3_scales[:],
+                rhs=hid_codes[:].bitcast(FP8X4),
+                rhs_scale=hid_scales[:],
+                start=True,
+                stop=True,
+            )
+            res_sb = work.tile([P, V], F32, tag="res_sb", name="res_sb%d" % h)
+            nc.scalar.activation(res_sb[:], res[:, 0:V], ACT.Copy)
+            nc.sync.dma_start(out[:, cols], res_sb[:])

@@ -31,8 +31,8 @@ def tile_picked_ytweed_ll_p_kernel(
     nc = tc.nc
     with ExitStack() as ctx:
         keep = ctx.enter_context(tc.tile_pool(name="keep", bufs=1))
-        stage = ctx.enter_context(tc.tile_pool(name="stage", bufs=2))
         work = ctx.enter_context(tc.tile_pool(name="work", bufs=2))
+        shared = ctx.enter_context(tc.tile_pool(name="shared", bufs=1))
         psum = ctx.enter_context(tc.psum_pool(name="psum", bufs=1))
 
         def bank(b, name):
@@ -41,41 +41,49 @@ def tile_picked_ytweed_ll_p_kernel(
         offs_sb = keep.tile([P, S // 16], U16, name="offs_sb")
         nc.sync.dma_start(offs_sb[:], offs)
 
+        unit_sb = shared.tile([P, PACK], F32, name="unit_sb", align_bytes=64, offset=0)
+        nc.sync.dma_start(unit_sb[:], unit.rearrange("(p t) o -> p (t o)", t=PACK))
+        neg_unit = keep.tile([P, PACK], F32, name="neg_unit")
+        nc.vector.tensor_scalar(
+            out=neg_unit[:], in0=unit_sb[:], scalar1=-1.0 / D, scalar2=None, op0=ALU.mult
+        )
+        pos_unit = keep.tile([P, PACK], F32, name="pos_unit")
+        nc.vector.tensor_scalar(
+            out=pos_unit[:], in0=unit_sb[:], scalar1=1.0 / D, scalar2=None, op0=ALU.mult
+        )
+
         scale_table = keep.tile([P, T], U8, tag="bytes", name="scale_table", align_bytes=64)
         nc.vector.memset(scale_table[:].bitcast(I32), 0)
         for q in range(4):
-            nc.scalar.dma_start(
+            queue = nc.scalar if q < 2 else nc.sync
+            queue.dma_start(
                 scale_table[32 * q : 32 * q + 4, :].bitcast(I32),
                 x_scales[0, 4 * q : 4 * q + 4, :].bitcast(I32),
             )
 
-        w2_raw = stage.tile([P, PACK, H], F32, tag="raw", name="w2_raw")
+        w2_raw = keep.tile([P, PACK, H], F32, tag="w_raw", name="w2_raw")
         nc.sync.dma_start(w2_raw[:], w2.rearrange("(p j) c -> p j c", j=PACK))
-        word_table = keep.tile([P, T], U32, tag="table", name="word_table", align_bytes=64)
+        ident = keep.tile([P, P], F32, name="ident")
+        make_identity(nc, ident[:])
+        word_table = shared.tile([P, T], U32, name="word_table", align_bytes=64, offset=0)
         nc.sync.dma_start(
             word_table[:].bitcast(I32), x_words[0].rearrange("p n t -> p (n t)").bitcast(I32)
         )
-        w1_raw = stage.tile([P, PACK, H], F32, tag="raw", name="w1_raw")
+        w1_raw = keep.tile([P, PACK, H], F32, tag="w_raw", name="w1_raw")
         nc.sync.dma_start(w1_raw[:], w1.rearrange("(p j) c -> p j c", j=PACK))
         seg_sb = keep.tile([P, U // 16], U16, name="seg_sb")
         nc.sync.dma_start(seg_sb[:], seg)
 
-        ident = keep.tile([P, P], F32, name="ident")
-        make_identity(nc, ident[:])
 
         grp_win = [keep.tile([P, WINDOW], F32, name="grp_win%d" % t) for t in range(PACK)]
         log_win = [keep.tile([P, WINDOW], F32, name="log_win%d" % t) for t in range(PACK)]
         for win in grp_win + log_win:
             nc.vector.memset(win[:, V:WINDOW], 0.0)
 
-        def quantize_dealt(raw, sign, name, tag):
-            grouped = keep.tile([P, H * PACK], BF16, tag=tag, name=name + "_bf", align_bytes=64)
-            nc.vector.tensor_scalar(
-                out=grouped[:].rearrange("p (t m j) -> p m j t", t=PACK, j=PACK),
-                in0=raw[:].rearrange("p j (m t) -> p m j t", t=PACK),
-                scalar1=sign,
-                scalar2=None,
-                op0=ALU.mult,
+        def quantize_dealt(raw, grouped, name):
+            nc.vector.tensor_copy(
+                grouped[:].rearrange("p (t m j) -> p m j t", t=PACK, j=PACK),
+                raw[:].rearrange("p j (m t) -> p m j t", t=PACK),
             )
             codes = keep.tile([P, H], U32, name=name + "_codes", align_bytes=64)
             scales = keep.tile([P, H], U8, name=name + "_scales", align_bytes=64)
@@ -89,7 +97,8 @@ def tile_picked_ytweed_ll_p_kernel(
             x_sc[:].rearrange("p (b d v) -> p b v d", b=VB, d=D),
             picked_scales[:].rearrange("p (b v d) -> p b v d", b=VB, d=D),
         )
-        w2_codes, w2_scales = quantize_dealt(w2_raw, -1.0, "w2", "w2_bf")
+        w2_bf = keep.tile([P, H * PACK], BF16, name="w2_bf", align_bytes=64)
+        w2_codes, w2_scales = quantize_dealt(w2_raw, w2_bf, "w2")
         x_codes = keep.tile([P, S], U32, tag="picked", name="x_codes", align_bytes=64)
         x_cd = [x_codes[:, HALF * b : HALF * (b + 1)] for b in range(VB)]
         for b in range(VB):
@@ -97,51 +106,42 @@ def tile_picked_ytweed_ll_p_kernel(
                 x_cd[b].rearrange("p (d v) -> p v d", d=D),
                 word_table[:].indirect(offs_sb[:, 32 * b : 32 * (b + 1)]),
             )
-        w1_codes, w1_scales = quantize_dealt(w1_raw, 1.0, "w1", "table")
+        w1_bf = shared.tile([P, H * PACK], BF16, name="w1_bf", align_bytes=64, offset=0)
+        w1_codes, w1_scales = quantize_dealt(w1_raw, w1_bf, "w1")
 
-        exp_rows = exp_.rearrange("(p t) j -> p t j", t=PACK)
-        loss_rows = loss.rearrange("(p t) j -> p t j", t=PACK)
-        neg2e = [keep.tile([P, 2, S], F32, name="neg2e%d" % u) for u in range(2)]
-        for u in range(2):
-            exp_raw = stage.tile([P, 2, S], F32, tag="raw", name="exp_raw%d" % u)
-            nc.sync.dma_start(exp_raw[:], exp_rows[:, 2 * u : 2 * u + 2, :])
+        def deal(tile, raw, factor):
             nc.vector.tensor_scalar(
-                out=neg2e[u][:].rearrange("p t (b d v) -> p (t b) v d", b=VB, d=D),
-                in0=exp_raw[:].rearrange("p t (b v d) -> p (t b) v d", b=VB, d=D),
-                scalar1=-2.0,
+                out=tile[:].rearrange("p t (b d v) -> p (t b) v d", b=VB, d=D),
+                in0=raw[:].rearrange("p t (b v d) -> p (t b) v d", b=VB, d=D),
+                scalar1=factor,
                 scalar2=None,
                 op0=ALU.mult,
             )
-        loss_sb = []
+
+        exp_rows = exp_.rearrange("(p t) j -> p t j", t=PACK)
+        loss_rows = loss.rearrange("(p t) j -> p t j", t=PACK)
+        neg2e = []
         for u in range(2):
-            loss_raw = stage.tile([P, 2, S], F32, tag="raw", name="loss_raw%d" % u)
-            nc.sync.dma_start(loss_raw[:], loss_rows[:, 2 * u : 2 * u + 2, :])
-            loss_sb.append(loss_raw)
-        wt_sb = keep.tile([P, PACK, U], F32, tag="table", name="wt_sb", align_bytes=64)
+            raw = keep.tile([P, 2, S], F32, tag=("bytes", "w_raw")[u], name="exp_raw%d" % u, align_bytes=(64, None)[u])
+            nc.sync.dma_start(raw[:], exp_rows[:, 2 * u : 2 * u + 2, :])
+            dealt = shared.tile([P, 2, S], F32, name="neg2e%d" % u, align_bytes=64, offset=4096 + 8192 * u)
+            deal(dealt, raw, -2.0)
+            neg2e.append(dealt)
+        loss_raw = []
+        for u in range(2):
+            raw = keep.tile([P, 2, S], F32, tag=("bytes", "w_raw")[u], name="loss_raw%d" % u, align_bytes=(64, None)[u])
+            nc.sync.dma_start(raw[:], loss_rows[:, 2 * u : 2 * u + 2, :])
+            loss_raw.append(raw)
+        wt_sb = keep.tile([P, PACK, U], F32, tag="bytes", name="wt_sb", align_bytes=64)
         nc.sync.dma_start(wt_sb[:], wt.rearrange("(p t) r -> p t r", t=PACK))
-
-        unit_sb = keep.tile([P, PACK], F32, tag="w2_bf", name="unit_sb", align_bytes=64)
-        nc.sync.dma_start(unit_sb[:], unit.rearrange("(p t) o -> p (t o)", t=PACK))
-        w3_raw = keep.tile([P, PACK, N], F32, tag="bytes", name="w3_raw", align_bytes=64)
+        w3_raw = shared.tile([P, PACK, N], F32, name="w3_raw", align_bytes=64, offset=0)
         nc.sync.dma_start(w3_raw[:], w3.rearrange("(p j) c -> p j c", j=PACK))
-        w3_bf = keep.tile([P, N * PACK], BF16, name="w3_bf", align_bytes=64)
-        nc.vector.tensor_copy(
-            w3_bf[:].rearrange("p (c i j) -> p c j i", i=4, j=PACK),
-            w3_raw[:].rearrange("p j (c i) -> p c j i", i=4),
-        )
-        w3_codes = keep.tile([P, N], U32, name="w3_codes", align_bytes=64)
-        w3_scales = keep.tile([P, N], U8, name="w3_scales", align_bytes=64)
-        nc.vector.quantize_mx(out=w3_codes[:].bitcast(FP8X4), scales=w3_scales[:], in_=w3_bf[:])
-        neg_unit = keep.tile([P, PACK], F32, name="neg_unit")
-        nc.vector.tensor_scalar(
-            out=neg_unit[:], in0=unit_sb[:], scalar1=-1.0 / D, scalar2=None, op0=ALU.mult
-        )
 
-        neg_ph = {}
-        neg_disp = [keep.tile([P, D, H], F32, name="neg_disp%d" % b) for b in range(VB)]
+        ph = {}
+        neg_sp = [keep.tile([P, D, H], F32, tag="neg_sp%d" % b, name="neg_sp%d" % b) for b in range(VB)]
         for b in range(VB):
             for d in range(D):
-                acc = bank(D * b + d, "neg_ph%d%d" % (b, d))
+                acc = bank(D * b + d, "ph%d%d" % (b, d))
                 cols = slice(HALF * b + P * d, HALF * b + P * (d + 1))
                 nc.tensor.matmul_mx(
                     out=acc[:],
@@ -152,64 +152,62 @@ def tile_picked_ytweed_ll_p_kernel(
                     start=True,
                     stop=True,
                 )
-                nc.scalar.activation(neg_disp[b][:, d, :], acc[:], ACT.Sigmoid)
-                neg_ph[b, d] = acc
+                nc.scalar.activation(neg_sp[b][:, d, :], acc[:], ACT.Sigmoid, scale=-1.0)
+                ph[b, d] = acc
         for b in range(VB):
             for u in range(2):
-                pair = neg_disp[b][:, 2 * u : 2 * u + 2, :]
-                nc.scalar.activation(pair, pair, ACT.Ln, scale=math.exp(-0.3), bias=LN_FLOOR)
-        prod = keep.tile([P, VB, H], F32, tag="prod_tanh", name="prod")
-        pair_prod = []
+                pair = neg_sp[b][:, 2 * u : 2 * u + 2, :]
+                nc.scalar.activation(pair, pair, ACT.Ln, bias=LN_FLOOR)
         for b in range(VB):
             for d in range(D):
                 nc.vector.scalar_tensor_tensor(
-                    out=neg_disp[b][:, d, :],
-                    in0=neg_ph[b, d][:],
-                    scalar=-0.3,
-                    in1=neg_disp[b][:, d, :],
-                    op0=ALU.add,
+                    out=neg_sp[b][:, d, :],
+                    in0=ph[b, d][:],
+                    scalar=-1.0,
+                    in1=neg_sp[b][:, d, :],
+                    op0=ALU.mult,
                     op1=ALU.min,
                 )
-            other = keep.tile([P, 2, H], F32, name="other%d" % b)
-            for u in range(2):
-                nc.vector.tensor_tensor(
-                    other[:, 1 - u, :], neg_disp[b][:, 2 * u, :], neg_disp[b][:, 2 * u + 1, :], ALU.mult
-                )
-            nc.vector.tensor_tensor(prod[:, b, :], other[:, 0, :], other[:, 1, :], ALU.mult)
-            pair_prod.append(other)
-        log_prod = keep.tile([P, VB, H], F32, name="log_prod")
-        nc.scalar.activation(log_prod[:], prod[:], ACT.Ln)
-        cof = []
+        log_disp = keep.tile([P, VB * D, H], F32, name="log_disp")
         for b in range(VB):
-            cofactor = keep.tile([P, D, H], F32, name="cof%d" % b)
-            for e in range(2):
-                nc.vector.tensor_tensor(
-                    cofactor[:, e:D:2, :], neg_disp[b][:, 1 - e : D : 2, :], pair_prod[b][:], ALU.mult
-                )
-            cof.append(cofactor)
-
-        inv_prod = keep.tile([P, PACK, V], F32, name="inv_prod")
-        for u in range(2):
-            turned = bank(2 + u, "log_turned%d" % u)
-            for tt in range(2):
-                t = 2 * u + tt
-                for b in range(VB):
-                    nc.tensor.transpose(
-                        turned[:, V * tt + P * b : V * tt + P * (b + 1)],
-                        log_prod[:, b, P * t : P * (t + 1)],
-                        ident[:],
-                    )
-            for tt in range(2):
-                nc.scalar.activation(
-                    log_win[2 * u + tt][:, 0:V], turned[:, V * tt : V * (tt + 1)], ACT.Copy
-                )
             nc.scalar.activation(
-                inv_prod[:, 2 * u : 2 * u + 2, :].rearrange("p t v -> p (t v)"), turned[:], ACT.Exp, scale=-1.0
+                log_disp[:, D * b : D * (b + 1), :], neg_sp[b][:], ACT.Ln, scale=-1.0, bias=0.3
             )
 
-        hid = keep.tile([P, PACK, U], F32, name="hid")
+        loss_sb = []
+        for u in range(2):
+            dealt = keep.tile([P, 2, S], F32, name="loss%d" % u)
+            deal(dealt, loss_raw[u], 1.0)
+            loss_sb.append(dealt)
+        w3_bf = keep.tile([P, N * PACK], BF16, name="w3_bf", align_bytes=64)
+        nc.vector.tensor_copy(
+            w3_bf[:].rearrange("p (c i j) -> p c j i", i=4, j=PACK),
+            w3_raw[:].rearrange("p j (c i) -> p c j i", i=4),
+        )
+        w3_codes = keep.tile([P, N], U32, name="w3_codes", align_bytes=64)
+        w3_scales = keep.tile([P, N], U8, name="w3_scales", align_bytes=64)
+        nc.vector.quantize_mx(out=w3_codes[:].bitcast(FP8X4), scales=w3_scales[:], in_=w3_bf[:])
+
+        def turn_and_add(acc, terms):
+            for k, term in enumerate(terms):
+                nc.tensor.matmul(
+                    acc, lhsT=term, rhs=ident[:], start=(k == 0), stop=(k == len(terms) - 1), is_transpose=True
+                )
+
+        log_sums = [bank(4 + u, "log_sums%d" % u) for u in range(2)]
+        for b in range(VB):
+            for t in range(PACK):
+                first = V * (t % 2) + P * b
+                turn_and_add(
+                    log_sums[t // 2][:, first : first + P],
+                    [log_disp[:, D * b + d, P * t : P * (t + 1)] for d in range(D)],
+                )
+
+        devi_banks = [(2, 3), (6, 7), (4, 5), (3, 2)]
+        sums_banks = [2, 6, 4, 7]
+        inv_disp = []
         for t in range(PACK):
-            th = keep.tile([P, S], F32, tag="prod_tanh", name="th%d" % t)
+            th = keep.tile([P, S], F32, tag="neg_sp1", name="th%d" % t)
             for b in range(VB):
                 mu = bank(b, "mu%d%d" % (t, b))
                 nc.tensor.matmul_mx(
@@ -224,87 +222,82 @@ def tile_picked_ytweed_ll_p_kernel(
                 nc.scalar.activation(th[:, HALF * b : HALF * (b + 1)], mu[:], ACT.Tanh)
             inv_root = work.tile([P, S], F32, tag="inv_root", name="inv_root%d" % t)
             root = work.tile([P, S], F32, tag="root", name="root%d" % t)
-            nc.scalar.activation(inv_root[:], th[:], ACT.Exp, scale=-0.8)
-            nc.scalar.activation(root[:], th[:], ACT.Exp, scale=0.8)
-            logs = work.tile([P, U], F32, tag="logs", name="logs%d" % t)
-            for h in range(2):
-                nc.scalar.activation(
-                    logs[:, V * h : V * (h + 1)],
-                    log_win[t][:].indirect(seg_sb[:, 16 * h : 16 * (h + 1)]),
-                    ACT.Copy,
-                )
+            for b in range(VB):
+                half = slice(HALF * b, HALF * (b + 1))
+                nc.scalar.activation(inv_root[:, half], th[:, half], ACT.Exp, scale=-0.8)
+                nc.scalar.activation(root[:, half], th[:, half], ACT.Exp, scale=0.8)
+            for ahead in range(len(inv_disp), min(t + 2, PACK)):
+                tile = keep.tile([P, VB * D, P], F32, name="inv_disp%d" % ahead)
+                nc.scalar.activation(tile[:], log_disp[:, :, P * ahead : P * (ahead + 1)], ACT.Exp, scale=-1.0)
+                inv_disp.append(tile)
 
             ratio = work.tile([P, S], F32, tag="ratio", name="ratio%d" % t)
-            sums = bank(6 + t % 2, "sums%d" % t)
             for b in range(VB):
                 half = slice(HALF * b, HALF * (b + 1))
                 nc.vector.tensor_tensor(
-                    ratio[:, half].rearrange("p (d c i) -> p c d i", d=D, i=4),
-                    loss_sb[t // 2][:, t % 2, half].rearrange("p (c i d) -> p c d i", d=D, i=4),
-                    inv_root[:, half].rearrange("p (d c i) -> p c d i", d=D, i=4),
-                    ALU.mult,
+                    ratio[:, half], loss_sb[t // 2][:, t % 2, half], inv_root[:, half], ALU.mult
                 )
+            if t == 0:
+                for tt in range(PACK):
+                    nc.vector.tensor_scalar(
+                        out=log_win[tt][:, 0:V],
+                        in0=log_sums[tt // 2][:, V * (tt % 2) : V * (tt % 2 + 1)],
+                        scalar1=neg_unit[:, tt : tt + 1],
+                        scalar2=None,
+                        op0=ALU.mult,
+                    )
+            devi = [bank(devi_banks[t][b], "devi%d%d" % (t, b)) for b in range(VB)]
+            terms = [neg2e[t // 2][:, t % 2, :], ratio[:], root[:]]
             for b in range(VB):
-                devi = bank(4 - 2 * (t % 2) + b, "devi%d%d" % (t, b))
-                terms = [neg2e[t // 2][:, t % 2, :], root[:], ratio[:]]
                 for k, term in enumerate(terms):
                     for d in range(D):
                         nc.tensor.matmul(
-                            devi[:, P * d : P * (d + 1)],
+                            devi[b][:, P * d : P * (d + 1)],
                             lhsT=term[:, HALF * b + P * d : HALF * b + P * (d + 1)],
                             rhs=ident[:],
                             start=(k == 0 and d == 0),
                             stop=(k == len(terms) - 1 and d == D - 1),
                             is_transpose=True,
                         )
-                weighted = work.tile([P, D, P], F32, tag="weighted", name="weighted%d%d" % (t, b))
+            weighted = []
+            for b in range(VB):
+                tile = work.tile([P, D, P], F32, tag="weighted", name="weighted%d%d" % (t, b))
                 nc.vector.tensor_tensor(
-                    weighted[:],
-                    devi[:].rearrange("p (d i) -> p d i", d=D),
-                    cof[b][:, :, P * t : P * (t + 1)],
+                    tile[:],
+                    devi[b][:].rearrange("p (d i) -> p d i", d=D),
+                    inv_disp[t][:, D * b : D * (b + 1), :],
                     ALU.mult,
                 )
-                for d in range(D):
-                    nc.tensor.matmul(
-                        sums[:, P * b : P * (b + 1)],
-                        lhsT=weighted[:, d, :],
-                        rhs=ident[:],
-                        start=(d == 0),
-                        stop=(d == D - 1),
-                        is_transpose=True,
-                    )
-            nc.vector.scalar_tensor_tensor(
+                weighted.append(tile)
+            sums = bank(sums_banks[t], "sums%d" % t)
+            for b in range(VB):
+                turn_and_add(sums[:, P * b : P * (b + 1)], [weighted[b][:, d, :] for d in range(D)])
+            nc.vector.tensor_scalar(
                 out=grp_win[t][:, 0:V],
                 in0=sums[:, 0:V],
-                scalar=neg_unit[:, t : t + 1],
-                in1=inv_prod[:, t, :],
+                scalar1=pos_unit[:, t : t + 1],
+                scalar2=None,
                 op0=ALU.mult,
-                op1=ALU.mult,
             )
-            scaled = work.tile([P, U], F32, tag="scaled", name="scaled%d" % t)
+
+        hid = keep.tile([P, PACK, U], F32, name="hid")
+        for t in range(PACK):
+            scaled = keep.tile([P, U], F32, name="scaled%d" % t)
+            logs = keep.tile([P, U], F32, name="logs%d" % t)
             for h in range(2):
                 cols = slice(V * h, V * (h + 1))
+                picks = seg_sb[:, 16 * h : 16 * (h + 1)]
                 nc.vector.tensor_tensor(
-                    scaled[:, cols],
-                    grp_win[t][:].indirect(seg_sb[:, 16 * h : 16 * (h + 1)]),
-                    wt_sb[:, t, cols],
-                    ALU.mult,
+                    scaled[:, cols], grp_win[t][:].indirect(picks), wt_sb[:, t, cols], ALU.mult
                 )
-            for h in range(2):
-                cols = slice(V * h, V * (h + 1))
-                nc.vector.scalar_tensor_tensor(
-                    out=hid[:, t, cols],
-                    in0=logs[:, cols],
-                    scalar=neg_unit[:, t : t + 1],
-                    in1=scaled[:, cols],
-                    op0=ALU.mult,
-                    op1=ALU.add,
-                )
+                nc.scalar.activation(logs[:, cols], log_win[t][:].indirect(picks), ACT.Copy)
+                nc.vector.tensor_tensor(hid[:, t, cols], logs[:, cols], scaled[:, cols], ALU.add)
 
         for h in range(2):
             cols = slice(V * h, V * (h + 1))
             hid_bf = work.tile([P, V * PACK], BF16, tag="hid_bf", name="hid_bf%d" % h, align_bytes=64)
-            nc.vector.tensor_copy(
+            weave = nc.scalar.copy if h == 0 else nc.vector.tensor_copy
+            weave(
                 hid_bf[:].rearrange("p (c i t) -> p c t i", i=4, t=PACK),
                 hid[:, :, cols].rearrange("p t (c i) -> p c t i", i=4),
             )

@@ -94,8 +94,8 @@ def tile_picked_ytweed_ll_p_kernel(
         nc.vector.tensor_copy(picked_scales[:], scale_table[:].indirect(offs_sb[:]))
         x_sc = keep.tile([P, S], U8, name="x_sc", align_bytes=64)
         nc.vector.tensor_copy(
-            x_sc[:].rearrange("p (b d v) -> p b v d", b=VB, d=D),
-            picked_scales[:].rearrange("p (b v d) -> p b v d", b=VB, d=D),
+            x_sc[:].rearrange("p (b d v) -> p b d v", b=VB, d=D),
+            picked_scales[:].rearrange("p (b v d) -> p b d v", b=VB, d=D),
         )
         w2_bf = keep.tile([P, H * PACK], BF16, name="w2_bf", align_bytes=64)
         w2_codes, w2_scales = quantize_dealt(w2_raw, w2_bf, "w2")
@@ -205,70 +205,76 @@ def tile_picked_ytweed_ll_p_kernel(
 
         devi_banks = [(2, 3), (6, 7), (4, 5), (3, 2)]
         sums_banks = [2, 6, 4, 7]
-        inv_disp = []
-        for t in range(PACK):
-            th = keep.tile([P, S], F32, tag="neg_sp1", name="th%d" % t)
-            for b in range(VB):
-                mu = bank(b, "mu%d%d" % (t, b))
-                nc.tensor.matmul_mx(
-                    out=mu[:],
-                    lhsT=w1_codes[:, P * t : P * (t + 1)].bitcast(FP8X4),
-                    lhsT_scale=w1_scales[:, P * t : P * (t + 1)],
-                    rhs=x_cd[b].bitcast(FP8X4),
-                    rhs_scale=x_sc[:, HALF * b : HALF * (b + 1)],
-                    start=True,
-                    stop=True,
-                )
-                nc.scalar.activation(th[:, HALF * b : HALF * (b + 1)], mu[:], ACT.Tanh)
-            inv_root = work.tile([P, S], F32, tag="inv_root", name="inv_root%d" % t)
-            root = work.tile([P, S], F32, tag="root", name="root%d" % t)
-            for b in range(VB):
-                half = slice(HALF * b, HALF * (b + 1))
-                nc.scalar.activation(inv_root[:, half], th[:, half], ACT.Exp, scale=-0.8)
-                nc.scalar.activation(root[:, half], th[:, half], ACT.Exp, scale=0.8)
-            for ahead in range(len(inv_disp), min(t + 2, PACK)):
-                tile = keep.tile([P, VB * D, P], F32, name="inv_disp%d" % ahead)
-                nc.scalar.activation(tile[:], log_disp[:, :, P * ahead : P * (ahead + 1)], ACT.Exp, scale=-1.0)
-                inv_disp.append(tile)
+        inv_disp = {}
 
-            ratio = work.tile([P, S], F32, tag="ratio", name="ratio%d" % t)
+        def invert(t, b):
+            tile = keep.tile([P, D, P], F32, name="inv_disp%d%d" % (t, b))
+            nc.scalar.activation(
+                tile[:], log_disp[:, D * b : D * (b + 1), P * t : P * (t + 1)], ACT.Exp, scale=-1.0
+            )
+            inv_disp[t, b] = tile
+
+        def bounded_mean(t, b):
+            mu = bank(b, "mu%d%d" % (t, b))
+            nc.tensor.matmul_mx(
+                out=mu[:],
+                lhsT=w1_codes[:, P * t : P * (t + 1)].bitcast(FP8X4),
+                lhsT_scale=w1_scales[:, P * t : P * (t + 1)],
+                rhs=x_cd[b].bitcast(FP8X4),
+                rhs_scale=x_sc[:, HALF * b : HALF * (b + 1)],
+                start=True,
+                stop=True,
+            )
+            th = keep.tile([P, HALF], F32, tag="neg_sp%d" % (1 - b), name="th%d%d" % (t, b))
+            nc.scalar.activation(th[:], mu[:], ACT.Tanh)
+            return th
+
+        bounded = [bounded_mean(0, 0)]
+        logs = [keep.tile([P, U], F32, name="logs%d" % t) for t in range(PACK)]
+        for t in range(PACK):
+            weighted = []
             for b in range(VB):
                 half = slice(HALF * b, HALF * (b + 1))
-                nc.vector.tensor_tensor(
-                    ratio[:, half], loss_sb[t // 2][:, t % 2, half], inv_root[:, half], ALU.mult
-                )
-            if t == 0:
-                for tt in range(PACK):
-                    nc.vector.tensor_scalar(
-                        out=log_win[tt][:, 0:V],
-                        in0=log_sums[tt // 2][:, V * (tt % 2) : V * (tt % 2 + 1)],
-                        scalar1=neg_unit[:, tt : tt + 1],
-                        scalar2=None,
-                        op0=ALU.mult,
-                    )
-            devi = [bank(devi_banks[t][b], "devi%d%d" % (t, b)) for b in range(VB)]
-            terms = [neg2e[t // 2][:, t % 2, :], ratio[:], root[:]]
-            for b in range(VB):
+                if VB * t + b + 1 < VB * PACK:
+                    bounded.append(bounded_mean(*divmod(VB * t + b + 1, VB)))
+                th = bounded[VB * t + b]
+                inv_root = work.tile([P, HALF], F32, tag="inv_root", name="inv_root%d%d" % (t, b), bufs=3)
+                root = work.tile([P, HALF], F32, tag="root", name="root%d%d" % (t, b), bufs=3)
+                nc.scalar.activation(inv_root[:], th[:], ACT.Exp, scale=-0.8)
+                nc.scalar.activation(root[:], th[:], ACT.Exp, scale=0.8)
+                if t == 0:
+                    invert(0, b)
+                if t + 1 < PACK:
+                    invert(t + 1, b)
+
+                ratio = work.tile([P, HALF], F32, tag="ratio", name="ratio%d%d" % (t, b), bufs=3)
+                nc.vector.tensor_tensor(ratio[:], loss_sb[t // 2][:, t % 2, half], inv_root[:], ALU.mult)
+                devi = bank(devi_banks[t][b], "devi%d%d" % (t, b))
+                terms = [neg2e[t // 2][:, t % 2, half], root[:], ratio[:]]
                 for k, term in enumerate(terms):
                     for d in range(D):
                         nc.tensor.matmul(
-                            devi[b][:, P * d : P * (d + 1)],
-                            lhsT=term[:, HALF * b + P * d : HALF * b + P * (d + 1)],
+                            devi[:, P * d : P * (d + 1)],
+                            lhsT=term[:, P * d : P * (d + 1)],
                             rhs=ident[:],
                             start=(k == 0 and d == 0),
                             stop=(k == len(terms) - 1 and d == D - 1),
                             is_transpose=True,
                         )
-            weighted = []
-            for b in range(VB):
-                tile = work.tile([P, D, P], F32, tag="weighted", name="weighted%d%d" % (t, b))
+                tile = work.tile([P, D, P], F32, tag="weighted", name="weighted%d%d" % (t, b), bufs=3)
                 nc.vector.tensor_tensor(
-                    tile[:],
-                    devi[b][:].rearrange("p (d i) -> p d i", d=D),
-                    inv_disp[t][:, D * b : D * (b + 1), :],
-                    ALU.mult,
+                    tile[:], devi[:].rearrange("p (d i) -> p d i", d=D), inv_disp[t, b][:], ALU.mult
                 )
                 weighted.append(tile)
+                if t == 0 and b == 0:
+                    for tt in range(PACK):
+                        nc.vector.tensor_scalar(
+                            out=log_win[tt][:, 0:V],
+                            in0=log_sums[tt // 2][:, V * (tt % 2) : V * (tt % 2 + 1)],
+                            scalar1=neg_unit[:, tt : tt + 1],
+                            scalar2=None,
+                            op0=ALU.mult,
+                        )
             sums = bank(sums_banks[t], "sums%d" % t)
             for b in range(VB):
                 turn_and_add(sums[:, P * b : P * (b + 1)], [weighted[b][:, d, :] for d in range(D)])
@@ -283,15 +289,14 @@ def tile_picked_ytweed_ll_p_kernel(
         hid = keep.tile([P, PACK, U], F32, name="hid")
         for t in range(PACK):
             scaled = keep.tile([P, U], F32, name="scaled%d" % t)
-            logs = keep.tile([P, U], F32, name="logs%d" % t)
             for h in range(2):
                 cols = slice(V * h, V * (h + 1))
                 picks = seg_sb[:, 16 * h : 16 * (h + 1)]
                 nc.vector.tensor_tensor(
                     scaled[:, cols], grp_win[t][:].indirect(picks), wt_sb[:, t, cols], ALU.mult
                 )
-                nc.scalar.activation(logs[:, cols], log_win[t][:].indirect(picks), ACT.Copy)
-                nc.vector.tensor_tensor(hid[:, t, cols], logs[:, cols], scaled[:, cols], ALU.add)
+                nc.scalar.activation(logs[t][:, cols], log_win[t][:].indirect(picks), ACT.Copy)
+                nc.vector.tensor_tensor(hid[:, t, cols], logs[t][:, cols], scaled[:, cols], ALU.add)
 
         for h in range(2):
             cols = slice(V * h, V * (h + 1))

@@ -205,14 +205,6 @@ def tile_picked_ytweed_ll_p_kernel(
 
         devi_banks = [(2, 3), (6, 7), (4, 5), (3, 2)]
         sums_banks = [2, 6, 4, 7]
-        inv_disp = {}
-
-        def invert(t, b):
-            tile = keep.tile([P, D, P], F32, name="inv_disp%d%d" % (t, b))
-            nc.scalar.activation(
-                tile[:], log_disp[:, D * b : D * (b + 1), P * t : P * (t + 1)], ACT.Exp, scale=-1.0
-            )
-            inv_disp[t, b] = tile
 
         def bounded_mean(t, b):
             mu = bank(b, "mu%d%d" % (t, b))
@@ -229,82 +221,96 @@ def tile_picked_ytweed_ll_p_kernel(
             nc.scalar.activation(th[:], mu[:], ACT.Tanh)
             return th
 
-        bounded = [bounded_mean(0, 0)]
-        logs = [keep.tile([P, U], F32, name="logs%d" % t) for t in range(PACK)]
-        for t in range(PACK):
-            weighted = []
-            for b in range(VB):
-                half = slice(HALF * b, HALF * (b + 1))
-                if VB * t + b + 1 < VB * PACK:
-                    bounded.append(bounded_mean(*divmod(VB * t + b + 1, VB)))
-                th = bounded[VB * t + b]
-                inv_root = work.tile([P, HALF], F32, tag="inv_root", name="inv_root%d%d" % (t, b), bufs=3)
-                root = work.tile([P, HALF], F32, tag="root", name="root%d%d" % (t, b), bufs=3)
-                nc.scalar.activation(inv_root[:], th[:], ACT.Exp, scale=-0.8)
-                nc.scalar.activation(root[:], th[:], ACT.Exp, scale=0.8)
-                if t == 0:
-                    invert(0, b)
-                if t + 1 < PACK:
-                    invert(t + 1, b)
+        def deviance(t, b, th):
+            half = slice(HALF * b, HALF * (b + 1))
+            inv_root = work.tile([P, HALF], F32, tag="inv_root", name="inv_root%d%d" % (t, b), bufs=3)
+            root = work.tile([P, HALF], F32, tag="root", name="root%d%d" % (t, b), bufs=3)
+            nc.scalar.activation(inv_root[:], th[:], ACT.Exp, scale=-0.8)
+            nc.scalar.activation(root[:], th[:], ACT.Exp, scale=0.8)
+            ratio = work.tile([P, HALF], F32, tag="ratio", name="ratio%d%d" % (t, b), bufs=3)
+            nc.vector.tensor_tensor(ratio[:], loss_sb[t // 2][:, t % 2, half], inv_root[:], ALU.mult)
+            devi = bank(devi_banks[t][b], "devi%d%d" % (t, b))
+            terms = [neg2e[t // 2][:, t % 2, half], root[:], ratio[:]]
+            for k, term in enumerate(terms):
+                for d in range(D):
+                    nc.tensor.matmul(
+                        devi[:, P * d : P * (d + 1)],
+                        lhsT=term[:, P * d : P * (d + 1)],
+                        rhs=ident[:],
+                        start=(k == 0 and d == 0),
+                        stop=(k == len(terms) - 1 and d == D - 1),
+                        is_transpose=True,
+                    )
+            return devi
 
-                ratio = work.tile([P, HALF], F32, tag="ratio", name="ratio%d%d" % (t, b), bufs=3)
-                nc.vector.tensor_tensor(ratio[:], loss_sb[t // 2][:, t % 2, half], inv_root[:], ALU.mult)
-                devi = bank(devi_banks[t][b], "devi%d%d" % (t, b))
-                terms = [neg2e[t // 2][:, t % 2, half], root[:], ratio[:]]
-                for k, term in enumerate(terms):
-                    for d in range(D):
-                        nc.tensor.matmul(
-                            devi[:, P * d : P * (d + 1)],
-                            lhsT=term[:, P * d : P * (d + 1)],
-                            rhs=ident[:],
-                            start=(k == 0 and d == 0),
-                            stop=(k == len(terms) - 1 and d == D - 1),
-                            is_transpose=True,
-                        )
-                tile = work.tile([P, D, P], F32, tag="weighted", name="weighted%d%d" % (t, b), bufs=3)
-                nc.vector.tensor_tensor(
-                    tile[:], devi[:].rearrange("p (d i) -> p d i", d=D), inv_disp[t, b][:], ALU.mult
-                )
-                weighted.append(tile)
-                if t == 0 and b == 0:
-                    for tt in range(PACK):
-                        nc.vector.tensor_scalar(
-                            out=log_win[tt][:, 0:V],
-                            in0=log_sums[tt // 2][:, V * (tt % 2) : V * (tt % 2 + 1)],
-                            scalar1=neg_unit[:, tt : tt + 1],
-                            scalar2=None,
-                            op0=ALU.mult,
-                        )
-            sums = bank(sums_banks[t], "sums%d" % t)
-            for b in range(VB):
-                turn_and_add(sums[:, P * b : P * (b + 1)], [weighted[b][:, d, :] for d in range(D)])
-            nc.vector.tensor_scalar(
-                out=grp_win[t][:, 0:V],
-                in0=sums[:, 0:V],
-                scalar1=pos_unit[:, t : t + 1],
-                scalar2=None,
-                op0=ALU.mult,
+        sums = {}
+
+        def group_mean(t, b, devi):
+            inv_disp = work.tile([P, D, P], F32, tag="inv_disp", name="inv_disp%d%d" % (t, b))
+            nc.scalar.activation(
+                inv_disp[:], log_disp[:, D * b : D * (b + 1), P * t : P * (t + 1)], ACT.Exp, scale=-1.0
             )
-
-        hid = keep.tile([P, PACK, U], F32, name="hid")
-        for t in range(PACK):
-            scaled = keep.tile([P, U], F32, name="scaled%d" % t)
-            for h in range(2):
-                cols = slice(V * h, V * (h + 1))
-                picks = seg_sb[:, 16 * h : 16 * (h + 1)]
-                nc.vector.tensor_tensor(
-                    scaled[:, cols], grp_win[t][:].indirect(picks), wt_sb[:, t, cols], ALU.mult
+            weighted = work.tile([P, D, P], F32, tag="weighted", name="weighted%d%d" % (t, b), bufs=3)
+            nc.vector.tensor_tensor(
+                weighted[:], devi[:].rearrange("p (d i) -> p d i", d=D), inv_disp[:], ALU.mult
+            )
+            if b == 0:
+                sums[t] = bank(sums_banks[t], "sums%d" % t)
+            groups = slice(P * b, P * (b + 1))
+            turn_and_add(sums[t][:, groups], [weighted[:, d, :] for d in range(D)])
+            if b == VB - 1:
+                nc.vector.tensor_scalar(
+                    out=grp_win[t][:, 0:V],
+                    in0=sums[t][:, 0:V],
+                    scalar1=pos_unit[:, t : t + 1],
+                    scalar2=None,
+                    op0=ALU.mult,
                 )
-                nc.scalar.activation(logs[t][:, cols], log_win[t][:].indirect(picks), ACT.Copy)
-                nc.vector.tensor_tensor(hid[:, t, cols], logs[t][:, cols], scaled[:, cols], ALU.add)
+
+        halves = [(t, b) for t in range(PACK) for b in range(VB)]
+        bounded = [bounded_mean(*halves[0])]
+        devis = []
+        for step, (t, b) in enumerate(halves):
+            if step + 1 < len(halves):
+                bounded.append(bounded_mean(*halves[step + 1]))
+            devis.append(deviance(t, b, bounded[step]))
+            if step == 0:
+                for tt in range(PACK):
+                    nc.vector.tensor_scalar(
+                        out=log_win[tt][:, 0:V],
+                        in0=log_sums[tt // 2][:, V * (tt % 2) : V * (tt % 2 + 1)],
+                        scalar1=neg_unit[:, tt : tt + 1],
+                        scalar2=None,
+                        op0=ALU.mult,
+                    )
+            else:
+                group_mean(*halves[step - 1], devis[step - 1])
+        group_mean(*halves[-1], devis[-1])
+
+        scaled = [keep.tile([P, PACK, V], F32, name="scaled%d" % h) for h in range(2)]
+        logs = [keep.tile([P, PACK, V], F32, name="logs%d" % h) for h in range(2)]
+        for h in range(2):
+            for t in range(PACK):
+                nc.scalar.activation(
+                    logs[h][:, t, :], log_win[t][:].indirect(seg_sb[:, 16 * h : 16 * (h + 1)]), ACT.Copy
+                )
+        for t in range(PACK):
+            for h in range(2):
+                nc.vector.tensor_tensor(
+                    scaled[h][:, t, :],
+                    grp_win[t][:].indirect(seg_sb[:, 16 * h : 16 * (h + 1)]),
+                    wt_sb[:, t, V * h : V * (h + 1)],
+                    ALU.mult,
+                )
 
         for h in range(2):
             cols = slice(V * h, V * (h + 1))
             hid_bf = work.tile([P, V * PACK], BF16, tag="hid_bf", name="hid_bf%d" % h, align_bytes=64)
-            weave = nc.scalar.copy if h == 0 else nc.vector.tensor_copy
-            weave(
+            nc.vector.tensor_tensor(
                 hid_bf[:].rearrange("p (c i t) -> p c t i", i=4, t=PACK),
-                hid[:, :, cols].rearrange("p t (c i) -> p c t i", i=4),
+                scaled[h][:].rearrange("p t (c i) -> p c t i", i=4),
+                logs[h][:].rearrange("p t (c i) -> p c t i", i=4),
+                ALU.add,
             )
             hid_codes = work.tile([P, V], U32, tag="hid_codes", name="hid_codes%d" % h, align_bytes=64)
             hid_scales = work.tile([P, V], U8, tag="hid_scales", name="hid_scales%d" % h, align_bytes=64)

import math
from contextlib import ExitStack

import concourse.mybir as mybir
from concourse.masks import make_identity

K, T, S, D, N, H, V, U = 512, 4096, 1024, 4, 128, 512, 256, 512
FLOPS = 2 * K * H * S * 2 + 2 * H * N * U

F32 = mybir.dt.float32
BF16 = mybir.dt.bfloat16
I32 = mybir.dt.int32
U32 = mybir.dt.uint32
U16 = mybir.dt.uint16
U8 = mybir.dt.uint8
FP8X4 = mybir.dt.float8_e4m3fn_x4
ALU = mybir.AluOpType
ACT = mybir.ActivationFunctionType

P = 128
PACK = 4
HALF = 512
VB = 2
WINDOW = V + 32
LN_FLOOR = 2.0 ** -60


def tile_picked_ytweed_ll_p_kernel(
    tc, x_words, x_scales, w1, w2, loss, exp_, wt, unit, w3, offs, seg, out
):
    nc = tc.nc
    with ExitStack() as ctx:
        keep = ctx.enter_context(tc.tile_pool(name="keep", bufs=1))
        work = ctx.enter_context(tc.tile_pool(name="work", bufs=2))
        shared = ctx.enter_context(tc.tile_pool(name="shared", bufs=1))
        psum = ctx.enter_context(tc.psum_pool(name="psum", bufs=1))

        def bank(b, name):
            return psum.tile([P, HALF], F32, tag="bank%d" % b, name=name)

        offs_sb = keep.tile([P, S // 16], U16, name="offs_sb")
        nc.sync.dma_start(offs_sb[:], offs)

        unit_sb = shared.tile([P, PACK], F32, name="unit_sb", align_bytes=64, offset=0)
        nc.sync.dma_start(unit_sb[:], unit.rearrange("(p t) o -> p (t o)", t=PACK))
        neg_unit = keep.tile([P, PACK], F32, name="neg_unit")
        nc.vector.tensor_scalar(
            out=neg_unit[:], in0=unit_sb[:], scalar1=-1.0 / D, scalar2=None, op0=ALU.mult
        )
        pos_unit = keep.tile([P, PACK], F32, name="pos_unit")
        nc.vector.tensor_scalar(
            out=pos_unit[:], in0=unit_sb[:], scalar1=1.0 / D, scalar2=None, op0=ALU.mult
        )

        scale_table = keep.tile([P, T], U8, tag="bytes", name="scale_table", align_bytes=64)
        nc.vector.memset(scale_table[:].bitcast(I32), 0)
        for q in range(4):
            queue = nc.scalar if q < 2 else nc.sync
            queue.dma_start(
                scale_table[32 * q : 32 * q + 4, :].bitcast(I32),
                x_scales[0, 4 * q : 4 * q + 4, :].bitcast(I32),
            )

        w2_raw = keep.tile([P, PACK, H], F32, tag="w_raw", name="w2_raw")
        nc.sync.dma_start(w2_raw[:], w2.rearrange("(p j) c -> p j c", j=PACK))
        ident = keep.tile([P, P], F32, name="ident")
        make_identity(nc, ident[:])
        word_table = shared.tile([P, T], U32, name="word_table", align_bytes=64, offset=0)
        nc.sync.dma_start(
            word_table[:].bitcast(I32), x_words[0].rearrange("p n t -> p (n t)").bitcast(I32)
        )
        w1_raw = keep.tile([P, PACK, H], F32, tag="w_raw", name="w1_raw")
        nc.sync.dma_start(w1_raw[:], w1.rearrange("(p j) c -> p j c", j=PACK))
        seg_sb = keep.tile([P, U // 16], U16, name="seg_sb")
        nc.sync.dma_start(seg_sb[:], seg)


        grp_win = [keep.tile([P, WINDOW], F32, name="grp_win%d" % t) for t in range(PACK)]
        log_win = [keep.tile([P, WINDOW], F32, name="log_win%d" % t) for t in range(PACK)]
        for win in grp_win + log_win:
            nc.vector.memset(win[:, V:WINDOW], 0.0)

        def quantize_dealt(raw, grouped, name):
            nc.vector.tensor_copy(
                grouped[:].rearrange("p (t m j) -> p m j t", t=PACK, j=PACK),
                raw[:].rearrange("p j (m t) -> p m j t", t=PACK),
            )
            codes = keep.tile([P, H], U32, name=name + "_codes", align_bytes=64)
            scales = keep.tile([P, H], U8, name=name + "_scales", align_bytes=64)
            nc.vector.quantize_mx(out=codes[:].bitcast(FP8X4), scales=scales[:], in_=grouped[:])
            return codes, scales

        picked_scales = keep.tile([P, S], U8, tag="picked", name="picked_scales", align_bytes=64)
        nc.vector.tensor_copy(picked_scales[:], scale_table[:].indirect(offs_sb[:]))
        x_sc = keep.tile([P, S], U8, name="x_sc", align_bytes=64)
        nc.vector.tensor_copy(
            x_sc[:].rearrange("p (b d v) -> p b d v", b=VB, d=D),
            picked_scales[:].rearrange("p (b v d) -> p b d v", b=VB, d=D),
        )
        w2_bf = keep.tile([P, H * PACK], BF16, name="w2_bf", align_bytes=64)
        w2_codes, w2_scales = quantize_dealt(w2_raw, w2_bf, "w2")
        x_codes = keep.tile([P, S], U32, tag="picked", name="x_codes", align_bytes=64)
        x_cd = [x_codes[:, HALF * b : HALF * (b + 1)] for b in range(VB)]
        for b in range(VB):
            nc.vector.tensor_copy(
                x_cd[b].rearrange("p (d v) -> p v d", d=D),
                word_table[:].indirect(offs_sb[:, 32 * b : 32 * (b + 1)]),
            )
        w1_bf = shared.tile([P, H * PACK], BF16, name="w1_bf", align_bytes=64, offset=0)
        w1_codes, w1_scales = quantize_dealt(w1_raw, w1_bf, "w1")

        def deal(tile, raw, factor):
            nc.vector.tensor_scalar(
                out=tile[:].rearrange("p t (b d v) -> p (t b) v d", b=VB, d=D),
                in0=raw[:].rearrange("p t (b v d) -> p (t b) v d", b=VB, d=D),
                scalar1=factor,
                scalar2=None,
                op0=ALU.mult,
            )

        exp_rows = exp_.rearrange("(p t) j -> p t j", t=PACK)
        loss_rows = loss.rearrange("(p t) j -> p t j", t=PACK)
        neg2e = []
        for u in range(2):
            raw = keep.tile([P, 2, S], F32, tag=("bytes", "w_raw")[u], name="exp_raw%d" % u, align_bytes=(64, None)[u])
            nc.sync.dma_start(raw[:], exp_rows[:, 2 * u : 2 * u + 2, :])
            dealt = shared.tile([P, 2, S], F32, name="neg2e%d" % u, align_bytes=64, offset=4096 + 8192 * u)
            deal(dealt, raw, -2.0)
            neg2e.append(dealt)
        loss_raw = []
        for u in range(2):
            raw = keep.tile([P, 2, S], F32, tag=("bytes", "w_raw")[u], name="loss_raw%d" % u, align_bytes=(64, None)[u])
            nc.sync.dma_start(raw[:], loss_rows[:, 2 * u : 2 * u + 2, :])
            loss_raw.append(raw)
        wt_sb = keep.tile([P, PACK, U], F32, tag="bytes", name="wt_sb", align_bytes=64)
        nc.sync.dma_start(wt_sb[:], wt.rearrange("(p t) r -> p t r", t=PACK))
        w3_raw = shared.tile([P, PACK, N], F32, name="w3_raw", align_bytes=64, offset=0)
        nc.sync.dma_start(w3_raw[:], w3.rearrange("(p j) c -> p j c", j=PACK))

        ph = {}
        neg_sp = [keep.tile([P, D, H], F32, tag="neg_sp%d" % b, name="neg_sp%d" % b) for b in range(VB)]
        for b in range(VB):
            for d in range(D):
                acc = bank(D * b + d, "ph%d%d" % (b, d))
                cols = slice(HALF * b + P * d, HALF * b + P * (d + 1))
                nc.tensor.matmul_mx(
                    out=acc[:],
                    lhsT=x_cd[b][:, P * d : P * (d + 1)].bitcast(FP8X4),
                    lhsT_scale=x_sc[:, cols],
                    rhs=w2_codes[:].bitcast(FP8X4),
                    rhs_scale=w2_scales[:],
                    start=True,
                    stop=True,
                )
                nc.scalar.activation(neg_sp[b][:, d, :], acc[:], ACT.Sigmoid, scale=-1.0)
                ph[b, d] = acc
        for b in range(VB):
            for u in range(2):
                pair = neg_sp[b][:, 2 * u : 2 * u + 2, :]
                nc.scalar.activation(pair, pair, ACT.Ln, bias=LN_FLOOR)
        for b in range(VB):
            for d in range(D):
                nc.vector.scalar_tensor_tensor(
                    out=neg_sp[b][:, d, :],
                    in0=ph[b, d][:],
                    scalar=-1.0,
                    in1=neg_sp[b][:, d, :],
                    op0=ALU.mult,
                    op1=ALU.min,
                )
        log_disp = keep.tile([P, VB * D, H], F32, name="log_disp")
        for b in range(VB):
            nc.scalar.activation(
                log_disp[:, D * b : D * (b + 1), :], neg_sp[b][:], ACT.Ln, scale=-1.0, bias=0.3
            )

        loss_sb = []
        for u in range(2):
            dealt = keep.tile([P, 2, S], F32, name="loss%d" % u)
            deal(dealt, loss_raw[u], 1.0)
            loss_sb.append(dealt)
        w3_bf = keep.tile([P, N * PACK], BF16, name="w3_bf", align_bytes=64)
        nc.vector.tensor_copy(
            w3_bf[:].rearrange("p (c i j) -> p c j i", i=4, j=PACK),
            w3_raw[:].rearrange("p j (c i) -> p c j i", i=4),
        )
        w3_codes = keep.tile([P, N], U32, name="w3_codes", align_bytes=64)
        w3_scales = keep.tile([P, N], U8, name="w3_scales", align_bytes=64)
        nc.vector.quantize_mx(out=w3_codes[:].bitcast(FP8X4), scales=w3_scales[:], in_=w3_bf[:])

        def turn_and_add(acc, terms):
            for k, term in enumerate(terms):
                nc.tensor.matmul(
                    acc, lhsT=term, rhs=ident[:], start=(k == 0), stop=(k == len(terms) - 1), is_transpose=True
                )

        log_sums = [bank(4 + u, "log_sums%d" % u) for u in range(2)]
        for b in range(VB):
            for t in range(PACK):
                first = V * (t % 2) + P * b
                turn_and_add(
                    log_sums[t // 2][:, first : first + P],
                    [log_disp[:, D * b + d, P * t : P * (t + 1)] for d in range(D)],
                )

        devi_banks = [(2, 3), (6, 7), (4, 5), (3, 2)]
        sums_banks = [2, 6, 4, 7]

        def bounded_mean(t, b):
            mu = bank(b, "mu%d%d" % (t, b))
            nc.tensor.matmul_mx(
                out=mu[:],
                lhsT=w1_codes[:, P * t : P * (t + 1)].bitcast(FP8X4),
                lhsT_scale=w1_scales[:, P * t : P * (t + 1)],
                rhs=x_cd[b].bitcast(FP8X4),
                rhs_scale=x_sc[:, HALF * b : HALF * (b + 1)],
                start=True,
                stop=True,
            )
            th = keep.tile([P, HALF], F32, tag="neg_sp%d" % (1 - b), name="th%d%d" % (t, b))
            nc.scalar.activation(th[:], mu[:], ACT.Tanh)
            return th

        def deviance(t, b, th):
            half = slice(HALF * b, HALF * (b + 1))
            inv_root = work.tile([P, HALF], F32, tag="inv_root", name="inv_root%d%d" % (t, b), bufs=3)
            root = work.tile([P, HALF], F32, tag="root", name="root%d%d" % (t, b), bufs=3)
            nc.scalar.activation(inv_root[:], th[:], ACT.Exp, scale=-0.8)
            nc.scalar.activation(root[:], th[:], ACT.Exp, scale=0.8)
            ratio = work.tile([P, HALF], F32, tag="ratio", name="ratio%d%d" % (t, b), bufs=3)
            nc.vector.tensor_tensor(ratio[:], loss_sb[t // 2][:, t % 2, half], inv_root[:], ALU.mult)
            devi = bank(devi_banks[t][b], "devi%d%d" % (t, b))
            terms = [neg2e[t // 2][:, t % 2, half], root[:], ratio[:]]
            for k, term in enumerate(terms):
                for d in range(D):
                    nc.tensor.matmul(
                        devi[:, P * d : P * (d + 1)],
                        lhsT=term[:, P * d : P * (d + 1)],
                        rhs=ident[:],
                        start=(k == 0 and d == 0),
                        stop=(k == len(terms) - 1 and d == D - 1),
                        is_transpose=True,
                    )
            return devi

        sums = {}

        def group_mean(t, b, devi):
            inv_disp = work.tile([P, D, P], F32, tag="inv_disp", name="inv_disp%d%d" % (t, b))
            nc.scalar.activation(
                inv_disp[:], log_disp[:, D * b : D * (b + 1), P * t : P * (t + 1)], ACT.Exp, scale=-1.0
            )
            weighted = work.tile([P, D, P], F32, tag="weighted", name="weighted%d%d" % (t, b), bufs=3)
            nc.vector.tensor_tensor(
                weighted[:], devi[:].rearrange("p (d i) -> p d i", d=D), inv_disp[:], ALU.mult
            )
            if b == 0:
                sums[t] = bank(sums_banks[t], "sums%d" % t)
            groups = slice(P * b, P * (b + 1))
            turn_and_add(sums[t][:, groups], [weighted[:, d, :] for d in range(D)])
            if b == VB - 1:
                nc.vector.tensor_scalar(
                    out=grp_win[t][:, 0:V],
                    in0=sums[t][:, 0:V],
                    scalar1=pos_unit[:, t : t + 1],
                    scalar2=None,
                    op0=ALU.mult,
                )

        halves = [(t, b) for t in range(PACK) for b in range(VB)]
        bounded = [bounded_mean(*halves[0])]
        devis = []
        for step, (t, b) in enumerate(halves):
            if step + 1 < len(halves):
                bounded.append(bounded_mean(*halves[step + 1]))
            devis.append(deviance(t, b, bounded[step]))
            if step == 0:
                for tt in range(PACK):
                    nc.vector.tensor_scalar(
                        out=log_win[tt][:, 0:V],
                        in0=log_sums[tt // 2][:, V * (tt % 2) : V * (tt % 2 + 1)],
                        scalar1=neg_unit[:, tt : tt + 1],
                        scalar2=None,
                        op0=ALU.mult,
                    )
            else:
                group_mean(*halves[step - 1], devis[step - 1])
        group_mean(*halves[-1], devis[-1])

        scaled = [keep.tile([P, PACK, V], F32, name="scaled%d" % h) for h in range(2)]
        logs = [keep.tile([P, PACK, V], F32, name="logs%d" % h) for h in range(2)]
        for h in range(2):
            for t in range(PACK):
                nc.scalar.activation(
                    logs[h][:, t, :], log_win[t][:].indirect(seg_sb[:, 16 * h : 16 * (h + 1)]), ACT.Copy
                )
        for t in range(PACK):
            for h in range(2):
                nc.vector.tensor_tensor(
                    scaled[h][:, t, :],
                    grp_win[t][:].indirect(seg_sb[:, 16 * h : 16 * (h + 1)]),
                    wt_sb[:, t, V * h : V * (h + 1)],
                    ALU.mult,
                )

        for h in range(2):
            cols = slice(V * h, V * (h + 1))
            hid_bf = work.tile([P, V * PACK], BF16, tag="hid_bf", name="hid_bf%d" % h, align_bytes=64)
            nc.vector.tensor_tensor(
                hid_bf[:].rearrange("p (c i t) -> p c t i", i=4, t=PACK),
                scaled[h][:].rearrange("p t (c i) -> p c t i", i=4),
                logs[h][:].rearrange("p t (c i) -> p c t i", i=4),
                ALU.add,
            )
            hid_codes = work.tile([P, V], U32, tag="hid_codes", name="hid_codes%d" % h, align_bytes=64)
            hid_scales = work.tile([P, V], U8, tag="hid_scales", name="hid_scales%d" % h, align_bytes=64)
            nc.vector.quantize_mx(out=hid_codes[:].bitcast(FP8X4), scales=hid_scales[:], in_=hid_bf[:])
            res = bank(h, "res%d" % h)
            nc.tensor.matmul_mx(
                out=res[:, 0:V],
                lhsT=w3_codes[:].bitcast(FP8X4),
                lhsT_scale=w3_scales[:],
                rhs=hid_codes[:].bitcast(FP8X4),
                rhs_scale=hid_scales[:],
                start=True,
                stop=True,
            )
            res_sb = work.tile([P, V], F32, tag="res_sb", name="res_sb%d" % h)
            nc.scalar.activation(res_sb[:], res[:, 0:V], ACT.Copy)
            nc.sync.dma_start(out[:, cols], res_sb[:])
